import numpy as np
import ml_dtypes


def mxq(x, axis, fmt="e4m3"):
    dtype, down = {"e4m3": (ml_dtypes.float8_e4m3fn, 7), "e5m2": (ml_dtypes.float8_e5m2, 14)}[fmt]
    v = np.moveaxis(np.asarray(x, np.float32).astype(ml_dtypes.bfloat16).astype(np.float64), axis, -1)
    blocks = v.reshape(v.shape[:-1] + (-1, 32))
    amax = np.abs(blocks).max(-1, keepdims=True)
    byte = np.maximum(np.where(amax > 0, np.frexp(amax)[1] - 1 + 127, 0) - down, 1)
    scale = np.exp2(byte - 127.0)
    codes = (blocks / scale).astype(np.float32).astype(dtype).astype(np.float64)
    return np.moveaxis((codes * scale).reshape(v.shape), -1, axis)


WIDE = False


def mx_kscale(k):
    if not WIDE:
        return np.ones(k)
    levels = np.array([10, -10, 5, -5, 0])
    if k % 512:
        return np.exp2(np.random.permutation(np.resize(levels, k // 32))).repeat(32)
    a = np.empty((k // 512, 16))
    for p in range(k // 512):
        a[p, :8] = np.random.permutation(np.resize(levels, 8))
        for g in range(8):
            far = levels[np.abs(levels - a[p, g]) >= 10]
            a[p, g + 8] = far[np.random.randint(len(far))]
    return np.exp2(a.ravel()).repeat(32)


def f64(x):
    return np.asarray(x).astype(np.float64)


def striped(idx):
    return np.tile(idx.reshape(-1, 16).T, (8, 1)).astype(np.uint16)


def unstriped(offs):
    return offs[:16].T.reshape(-1).astype(np.int64)


E2M1 = np.array([0.0, 0.5, 1.0, 1.5, 2.0, 3.0, 4.0, 6.0, -0.0, -0.5, -1.0, -1.5, -2.0, -3.0, -4.0, -6.0])


def pack_weight(w, fmt):
    k, n = w.shape
    w = f64(np.asarray(w, np.float32).astype(ml_dtypes.bfloat16)).reshape(k // 32, 32, n)
    amax = np.abs(w).max(1)
    if fmt == "e4m3":
        byte = np.frexp(amax)[1] - 1 + 127 - 7
    else:
        mant, ex = np.frexp(amax / 6.0)
        byte = np.where(mant > 0.5, ex, ex - 1) + 127
    byte = np.clip(np.where(amax > 0, byte, 1), 1, 254)
    scaled = (w * np.exp2(127.0 - byte)[:, None, :]).reshape(k, n).astype(np.float32)
    by_word = np.ascontiguousarray(scaled.reshape(k // 512, 128, 4, n).transpose(0, 1, 3, 2))
    if fmt == "e4m3":
        words = by_word.astype(ml_dtypes.float8_e4m3fn).view(np.uint8)
    else:
        c = by_word.astype(ml_dtypes.float4_e2m1fn).view(np.uint8) & 0xF
        words = (c[..., 0::2] | (c[..., 1::2] << 4)).reshape(k // 512, 128, 2 * n)
    return np.ascontiguousarray(words), np.ascontiguousarray(byte.astype(np.uint8).reshape(k // 512, 16, n))


def unpack_weight(words, scales, fmt):
    g, _, n = scales.shape
    words = np.ascontiguousarray(words).reshape(g, 128, n, -1)
    if fmt == "e4m3":
        vals = words.view(ml_dtypes.float8_e4m3fn).astype(np.float64)
    else:
        nib = np.empty((g, 128, n, 4), np.uint8)
        nib[..., 0::2] = words & 0xF
        nib[..., 1::2] = words >> 4
        vals = E2M1[nib]
    vals = vals * np.repeat(np.exp2(scales.astype(np.float64) - 127.0), 8, axis=1)[..., None]
    return vals.transpose(0, 1, 3, 2).reshape(g * 512, n)


def gelu(v):
    return 0.5 * v * (1.0 + np.tanh(np.sqrt(2.0 / np.pi) * (v + 0.044715 * v**3)))


def striped8(idx):
    return np.concatenate([v.reshape(-1, 16).T for v in idx]).astype(np.uint16)


def unstriped8(offs):
    return np.stack([offs[16 * g:16 * g + 16].T.reshape(-1) for g in range(8)]).astype(np.int64)


def heads(xT, wgt, idx8):
    k = np.arange(xT.shape[0])
    return wgt[k // 4 % 128] * xT[k[:, None], idx8[k % 512 // 64]]


K, D, T2, T, S, H, N = 1024, 512, 2048, 2048, 1024, 1024, 512

def setup_inputs():
    n = np.random.standard_normal
    s = mx_kscale(K)[:, None]
    d = mx_kscale(D)[:, None]
    u = mx_kscale(H)[:, None]
    xT = (n((K, T2)) * s).astype(np.float32)
    wgt = np.repeat(np.random.uniform(0.5, 2.0, (8, S)), 16, axis=0).astype(np.float32)
    offs2 = striped8(np.stack([np.random.permutation(T2)[:S] for _ in range(8)]))
    tab_words, tab_scales = pack_weight(n((D, T)) * d, "e4m3")
    offs = striped(np.random.permutation(T)[:S])
    we = (n((K, H)) / np.sqrt(K) / s).astype(np.float32)
    wr = (n((D, H)) / np.sqrt(D) / d * u.T).astype(np.float32)
    wp = (n((K, N)) / np.sqrt(K) / s).astype(np.float32)
    w4_words, w4_scales = pack_weight(n((H, N)) / np.sqrt(H) / u, "e2m1")
    b = (0.5 * n(N)).astype(np.float32)
    return dict(xT=xT, wgt=wgt, offs2=offs2, tab_words=tab_words, tab_scales=tab_scales, offs=offs,
                we=we, wr=wr, wp=wp, w4_words=w4_words, w4_scales=w4_scales, b=b)

def reference(xT, wgt, offs2, tab_words, tab_scales, offs, we, wr, wp, w4_words, w4_scales, b):
    xg = mxq(heads(f64(xT), f64(wgt), unstriped8(offs2)), 0, "e4m3")
    v = unpack_weight(tab_words, tab_scales, "e4m3")[:, unstriped(offs)]
    e = mxq(f64(we), 0, "e4m3").T @ xg
    r = mxq(f64(wr), 0, "e4m3").T @ v
    h = mxq(e * r, 0, "e4m3")
    w4 = unpack_weight(w4_words, w4_scales, "e2m1")
    z = w4.T @ h + mxq(f64(wp), 0, "e4m3").T @ xg
    z = z + f64(b)[:, None]
    return 1.0 / (1.0 + np.exp(-z))

@@ -1,0 +1,269 @@
+from contextlib import ExitStack
+
+import concourse.mybir as mybir
+
+K, D, T2, T, S, H, N = 1024, 512, 2048, 2048, 1024, 1024, 512
+FLOPS = 2 * S * (K * H + D * H + H * N + K * N)
+
+F32 = mybir.dt.float32
+BF16 = mybir.dt.bfloat16
+I32 = mybir.dt.int32
+U32 = mybir.dt.uint32
+U16 = mybir.dt.uint16
+U8 = mybir.dt.uint8
+FP8 = mybir.dt.float8_e4m3fn_x4
+FP4 = mybir.dt.float4_e2m1fn_x4
+MULT = mybir.AluOpType.mult
+SIGMOID = mybir.ActivationFunctionType.Sigmoid
+P = 128
+MODE = "TT"
+
+
+def tile_list_triple_tail_score_kernel(tc, xT, wgt, offs2, tab_words, tab_scales, offs,
+                                                 we, wr, wp, w4_words, w4_scales, b, out):
+    nc = tc.nc
+    with ExitStack() as ctx:
+        keep = ctx.enter_context(tc.tile_pool(name="keep", bufs=1))
+        xpool = ctx.enter_context(tc.tile_pool(name="xpool", bufs=6))
+        wpool = ctx.enter_context(tc.tile_pool(name="wpool", bufs=4))
+        psum = ctx.enter_context(tc.psum_pool(name="psum", bufs=1))
+
+        def kept(name, shape, dtype):
+            return keep.tile(shape, dtype, name=name, align_bytes=64)
+
+        rel_list = keep.tile([P, S // 16], U16, name="rel_list")
+        head_lists = keep.tile([P, S // 16], U16, name="head_lists")
+        tab_w = kept("tab_w", [P, T], I32)
+        tab_s = kept("tab_s", [P, T], U8)
+        v_w = kept("v_w", [P, S], U32)
+        v_s = kept("v_s", [P, S], U8)
+        wgt_sb = kept("wgt_sb", [P, S], F32)
+        w4_w = kept("w4_w", [P, 2, 2 * N], U8)
+        w4_s = kept("w4_s", [P, 2, N], U8)
+        bias = kept("bias", [P, 4], F32)
+        picked = [kept("picked%d" % a, [P, 4, S], F32) for a in range(2)]
+        x_stage = [kept("x_stage%d" % i, [P, 1024], BF16) for i in range(2)]
+        w_stage = [kept("w_stage%d" % i, [P, 2048], BF16) for i in range(2)]
+        h_stage = [kept("h_stage%d" % i, [P, 1024], BF16) for i in range(2)]
+        xq = {(a, hf): (kept("xw%d%d" % (a, hf), [P, 512], U32), kept("xs%d%d" % (a, hf), [P, 512], U8))
+              for a in range(2) for hf in range(2)}
+        hq = {(c, hf): (kept("hw%d%d" % (c, hf), [P, 512], U32), kept("hs%d%d" % (c, hf), [P, 512], U8))
+              for c in range(2) for hf in range(2)}
+        q_sb = {(c, tt): kept("q%d%d" % (c, tt), [P, 128, 4], F32) for c in range(2) for tt in range(8)}
+        banks = [psum.tile([P, 512], F32, name="bank%d" % i) for i in range(8)]
+        wq = {}
+        x_sb = {}
+        w_raw = {}
+        count = {"w": 0, "x": 0, "h": 0, "q": 0, "e": 0}
+
+        def nxt(key):
+            count[key] = count[key] + 1
+            return count[key] - 1
+
+        x_planes = xT.rearrange("(a p i) t -> a i p t", a=2, i=4)
+
+        def load_x(pl):
+            x_sb[pl] = xpool.tile([P, T2], F32, name="x_plane")
+            nc.sync.dma_start(out=x_sb[pl][:], in_=x_planes[pl // 4, pl % 4])
+
+        def load_w(name, src, a, c):
+            w_raw[name] = wpool.tile([P, 4, 512], F32, name="w_raw")
+            nc.sync.dma_start(out=w_raw[name][:],
+                              in_=src[512 * a:512 * (a + 1), 512 * c:512 * (c + 1)].rearrange("(p j) c -> p j c", j=4))
+
+        def quantize(dst, cols, src):
+            nc.vector.quantize_mx(out=dst[0][:, cols].bitcast(FP8), scales=dst[1][:, cols], in_=src)
+
+        def prep_w(name, permute):
+            st = w_stage[nxt("w") % 2]
+            raw = w_raw[name]
+            if permute:
+                nc.scalar.copy(out=st[:].rearrange("p (u v m j) -> p u m j v", u=2, v=2, j=4),
+                               in_=raw[:].rearrange("p j (m u v) -> p u m j v", u=2, v=2))
+            else:
+                nc.scalar.copy(out=st[:].rearrange("p (c i j) -> p c j i", i=4, j=4),
+                               in_=raw[:].rearrange("p j (c i) -> p c j i", i=4))
+            wq[name] = (kept(name + "_w", [P, 512], U32), kept(name + "_s", [P, 512], U8))
+            quantize(wq[name], slice(0, 512), st[:])
+
+        def gather_x(pl, j0, j1):
+            win = x_sb[pl][:].indirect(head_lists[:, j0 // 16:j1 // 16])
+            dst = picked[pl // 4][:, pl % 4, j0:j1]
+            if MODE == "C":
+                nc.vector.tensor_tensor(dst, win, wgt_sb[:, j0:j1], MULT)
+            else:
+                nc.vector.tensor_copy(dst, win)
+
+        def weigh(a, q):
+            st = x_stage[nxt("x") % 2]
+            cols = slice(256 * q, 256 * (q + 1))
+            src = picked[a][:, :, cols].rearrange("p t (c i) -> p c t i", i=4)
+            dst = st[:].rearrange("p (c i t) -> p c t i", i=4, t=4)
+            if MODE == "C":
+                nc.scalar.copy(out=dst, in_=src)
+            else:
+                w_b = wgt_sb[:, cols].rearrange("p (c i) -> p c i", i=4).unsqueeze(2).to_broadcast([P, 64, 4, 4])
+                nc.vector.tensor_tensor(dst, src, w_b, MULT)
+            return lambda: quantize(xq[a, q // 2], slice(256 * (q % 2), 256 * (q % 2 + 1)), st[:])
+
+        def mm(dst, lhs, lcols, rhs, rcols, start, stop):
+            nc.tensor.matmul_mx(out=dst, lhsT=lhs[0][:, lcols].bitcast(FP8), lhsT_scale=lhs[1][:, lcols],
+                                rhs=rhs[0][:, rcols].bitcast(FP8), rhs_scale=rhs[1][:, rcols], start=start, stop=stop)
+
+        def relation(c, tt):
+            bank = banks[nxt("q") % 8]
+            for t in range(4):
+                mm(bank[:, 128 * t:128 * (t + 1)], wq["wr%d" % c], slice(128 * t, 128 * (t + 1)),
+                   (v_w, v_s), slice(128 * tt, 128 * (tt + 1)), True, True)
+            nc.scalar.copy(out=q_sb[c, tt][:], in_=bank[:].rearrange("p (t n) -> p n t", t=4))
+
+        def entity(c, q):
+            st = h_stage[nxt("h") % 2]
+            for u in range(2):
+                tt = 2 * q + u
+                bank = banks[nxt("e") % 4]
+                rc = slice(128 * (tt % 4), 128 * (tt % 4 + 1))
+                for t in range(4):
+                    for a in range(2):
+                        mm(bank[:, 128 * t:128 * (t + 1)], wq["we%d%d" % (a, c)], slice(128 * t, 128 * (t + 1)),
+                           xq[a, tt // 4], rc, a == 0, a == 1)
+                nc.vector.tensor_tensor(st[:, 512 * u:512 * (u + 1)].rearrange("p (n t) -> p n t", t=4),
+                                        bank[:].rearrange("p (t n) -> p n t", t=4), q_sb[c, tt][:], MULT)
+            return lambda: quantize(hq[c, q // 2], slice(256 * (q % 2), 256 * (q % 2 + 1)), st[:])
+
+        def z_dst(j0, width, bank0, nt):
+            per = 512 // width
+            return banks[bank0 + nt // per][:, width * (nt % per):width * (nt % per + 1)]
+
+        def score_head(j0, width, bank0, a):
+            per = 512 // width
+            for nt in range(4):
+                mm(z_dst(j0, width, bank0, nt), wq["wp%d" % a], slice(128 * nt, 128 * (nt + 1)),
+                   xq[a, j0 // 512], slice(j0 % 512, j0 % 512 + width), a == 0 and nt % per == 0, False)
+
+        def score_tail(j0, width, bank0, c, nts):
+            per = 512 // width
+            step = 512 if width == 512 else 128
+            for nt in nts:
+                for s0 in range(0, width, step):
+                    rc = slice(j0 % 512 + s0, j0 % 512 + s0 + step)
+                    nc.tensor.matmul_mx(
+                        out=z_dst(j0, width, bank0, nt)[:, s0:s0 + step],
+                        lhsT=w4_w[:, c, 256 * nt:256 * (nt + 1)].bitcast(FP4),
+                        lhsT_scale=w4_s[:, c, 128 * nt:128 * (nt + 1)],
+                        rhs=hq[c, j0 // 512][0][:, rc].bitcast(FP8), rhs_scale=hq[c, j0 // 512][1][:, rc],
+                        start=False, stop=(c == 1 and nt % per == per - 1 and s0 + step == width))
+
+        out_v = out.rearrange("(c p) j -> p c j", p=P)
+
+        def finish(j0, width, bank0):
+            per = 512 // width
+            res = wpool.tile([P, 4, width], F32, name="w_raw")
+            for n0 in range(0, 4, 2):
+                score_tail(j0, width, bank0, 1, range(n0, n0 + 2))
+                for nt in range(n0, n0 + 2):
+                    nc.scalar.activation(out=res[:, nt, :], in_=z_dst(j0, width, bank0, nt), func=SIGMOID,
+                                         bias=bias[:, nt:nt + 1])
+                nc.sync.dma_start(out=out_v[:, n0:n0 + 2, j0:j0 + width], in_=res[:, n0:n0 + 2, :])
+
+        nc.gpsimd.memset(tab_s[:].bitcast(I32), 0)
+        nc.gpsimd.memset(w4_s[:].bitcast(I32), 0)
+
+        nc.sync.dma_start(rel_list[:], offs)
+        nc.sync.dma_start(out=tab_w[:], in_=tab_words[0].rearrange("p t i -> p (t i)").bitcast(I32))
+        nc.sync.dma_start(head_lists[:], offs2)
+
+        load_x(0)
+        for qd in range(4):
+            nc.sync.dma_start(out=tab_s[32 * qd:32 * qd + 4, :].bitcast(I32),
+                              in_=tab_scales[0, 4 * qd:4 * qd + 4, :].bitcast(I32))
+        load_w("wr0", wr, 0, 0)
+        load_x(1)
+        load_x(2)
+        load_x(3)
+        nc.sync.dma_start(out=wgt_sb[:], in_=wgt)
+        load_w("wr1", wr, 0, 1)
+        load_x(4)
+        load_w("we00", we, 0, 0)
+        load_x(5)
+
+        nc.vector.tensor_copy(v_w[:], tab_w[:].bitcast(U32).indirect(rel_list[:]))
+        gather_x(0, 0, S)
+        load_x(6)
+        nc.vector.tensor_copy(v_s[:], tab_s[:].indirect(rel_list[:]))
+        prep_w("wr0", True)
+        load_w("we10", we, 1, 0)
+        gather_x(1, 0, S)
+        load_x(7)
+        load_w("we01", we, 0, 1)
+        for tt in range(8):
+            relation(0, tt)
+        gather_x(2, 0, S)
+        gather_x(3, 0, S)
+        prep_w("wr1", True)
+        load_w("we11", we, 1, 1)
+        nc.sync.dma_start(out=w4_w[:].bitcast(I32), in_=w4_words.rearrange("a p c -> p a c").bitcast(I32))
+        for qd in range(4):
+            nc.sync.dma_start(out=w4_s[32 * qd:32 * qd + 4, :, :].bitcast(I32),
+                              in_=w4_scales[:, 4 * qd:4 * qd + 4, :].rearrange("a r n -> r a n").bitcast(I32))
+        with nc.allow_non_contiguous_dma(reason="one bias value a partition"):
+            nc.sync.dma_start(out=bias[:], in_=b.rearrange("(c p) -> p c", p=P))
+        q0 = weigh(0, 0)
+        q1 = weigh(0, 1)
+        q0()
+        q1()
+        for tt in range(8):
+            relation(1, tt)
+        gather_x(4, 0, S)
+        prep_w("we00", True)
+        load_w("wp0", wp, 0, 0)
+        gather_x(5, 0, S)
+        gather_x(6, 0, S)
+        prep_w("we10", True)
+        load_w("wp1", wp, 1, 0)
+        gather_x(7, 0, 512)
+        q0 = weigh(1, 0)
+        q1 = weigh(1, 1)
+        q0()
+        gather_x(7, 512, S)
+        q1()
+        prep_w("we01", True)
+        h0 = entity(0, 0)
+        q0 = weigh(0, 2)
+        h0()
+        h1 = entity(0, 1)
+        q0()
+        prep_w("we11", True)
+        q1 = weigh(1, 2)
+        h1()
+        q0 = weigh(0, 3)
+        q1()
+        h0 = entity(1, 0)
+        q0()
+        prep_w("wp0", False)
+        q1 = weigh(1, 3)
+        h0()
+        h1 = entity(1, 1)
+        q1()
+        prep_w("wp1", False)
+        h0 = entity(0, 2)
+        h1()
+        score_head(0, 512, 4, 0)
+        score_head(0, 512, 4, 1)
+        score_tail(0, 512, 4, 0, range(4))
+        h1 = entity(1, 2)
+        h0()
+        finish(0, 512, 4)
+        h0 = entity(0, 3)
+        h1()
+        score_head(512, 256, 4, 0)
+        score_head(512, 256, 4, 1)
+        score_tail(512, 256, 4, 0, range(4))
+        h1 = entity(1, 3)
+        h0()
+        finish(512, 256, 4)
+        score_head(768, 256, 6, 0)
+        score_head(768, 256, 6, 1)
+        score_tail(768, 256, 6, 0, range(4))
+        h1()
+        finish(768, 256, 6)

@@ -11,12 +11,21 @@ I32 = mybir.dt.int32
 U32 = mybir.dt.uint32
 U16 = mybir.dt.uint16
 U8 = mybir.dt.uint8
-FP8 = mybir.dt.float8_e4m3fn_x4
-FP4 = mybir.dt.float4_e2m1fn_x4
+FP8X4 = mybir.dt.float8_e4m3fn_x4
+FP4X4 = mybir.dt.float4_e2m1fn_x4
 MULT = mybir.AluOpType.mult
 SIGMOID = mybir.ActivationFunctionType.Sigmoid
+
 P = 128
-MODE = "TT"
+PACK = 4
+PASS = P * PACK
+BANK = 512
+TILE, QUARTER, HALF = 128, 256, 512
+LIST_ROWS = 16
+MX_ALIGN = 64
+DMA_ALIGN = 256
+X_BUFS = 7
+W_BUFS = 4
 
 
 def tile_list_triple_tail_score_kernel(tc, xT, wgt, offs2, tab_words, tab_scales, offs,
@@ -24,246 +33,259 @@ def tile_list_triple_tail_score_kernel(tc, xT, wgt, offs2, tab_words, tab_scales
     nc = tc.nc
     with ExitStack() as ctx:
         keep = ctx.enter_context(tc.tile_pool(name="keep", bufs=1))
-        xpool = ctx.enter_context(tc.tile_pool(name="xpool", bufs=6))
-        wpool = ctx.enter_context(tc.tile_pool(name="wpool", bufs=4))
+        x_pool = ctx.enter_context(tc.tile_pool(name="x_pool", bufs=X_BUFS))
+        w_pool = ctx.enter_context(tc.tile_pool(name="w_pool", bufs=W_BUFS))
         psum = ctx.enter_context(tc.psum_pool(name="psum", bufs=1))
 
-        def kept(name, shape, dtype):
-            return keep.tile(shape, dtype, name=name, align_bytes=64)
+        def kept(name, shape, dtype, align=MX_ALIGN):
+            return keep.tile(shape, dtype, name=name, align_bytes=align)
 
-        rel_list = keep.tile([P, S // 16], U16, name="rel_list")
-        head_lists = keep.tile([P, S // 16], U16, name="head_lists")
-        tab_w = kept("tab_w", [P, T], I32)
-        tab_s = kept("tab_s", [P, T], U8)
-        v_w = kept("v_w", [P, S], U32)
-        v_s = kept("v_s", [P, S], U8)
-        wgt_sb = kept("wgt_sb", [P, S], F32)
-        w4_w = kept("w4_w", [P, 2, 2 * N], U8)
-        w4_s = kept("w4_s", [P, 2, N], U8)
-        bias = kept("bias", [P, 4], F32)
-        picked = [kept("picked%d" % a, [P, 4, S], F32) for a in range(2)]
-        x_stage = [kept("x_stage%d" % i, [P, 1024], BF16) for i in range(2)]
-        w_stage = [kept("w_stage%d" % i, [P, 2048], BF16) for i in range(2)]
-        h_stage = [kept("h_stage%d" % i, [P, 1024], BF16) for i in range(2)]
-        xq = {(a, hf): (kept("xw%d%d" % (a, hf), [P, 512], U32), kept("xs%d%d" % (a, hf), [P, 512], U8))
-              for a in range(2) for hf in range(2)}
-        hq = {(c, hf): (kept("hw%d%d" % (c, hf), [P, 512], U32), kept("hs%d%d" % (c, hf), [P, 512], U8))
-              for c in range(2) for hf in range(2)}
-        q_sb = {(c, tt): kept("q%d%d" % (c, tt), [P, 128, 4], F32) for c in range(2) for tt in range(8)}
-        banks = [psum.tile([P, 512], F32, name="bank%d" % i) for i in range(8)]
-        wq = {}
+        def mx_operand(name, columns):
+            return kept(name + "_words", [P, columns], U32), kept(name + "_scales", [P, columns], U8)
+
+        relation_list = keep.tile([P, S // LIST_ROWS], U16, name="relation_list")
+        head_lists = keep.tile([P, S // LIST_ROWS], U16, name="head_lists")
+        table_words = kept("table_words", [P, T], I32, DMA_ALIGN)
+        table_scales = kept("table_scales", [P, T], U8)
+        v_mx = mx_operand("v", S)
+        wgt_sb = kept("wgt_sb", [P, S], F32, DMA_ALIGN)
+        w4_words_sb = kept("w4_words_sb", [P, 2, 2 * N], U8)
+        w4_scales_sb = kept("w4_scales_sb", [P, 2, N], U8)
+        bias = kept("bias", [P, N // P], F32)
+        xg_f32 = [kept("xg_f32_%d" % a, [P, PACK, S], F32) for a in range(2)]
+        xg_stage = [kept("xg_stage%d" % i, [P, PACK * QUARTER], BF16) for i in range(2)]
+        w_stage = [kept("w_stage%d" % i, [P, PACK * PASS], BF16) for i in range(2)]
+        h_stage = [kept("h_stage%d" % part, [P, PACK * HALF], BF16) for part in range(2)]
+        xg_mx = {(a, half): mx_operand("xg%d%d" % (a, half), HALF) for a in range(2) for half in range(2)}
+        h_mx = {(part, half): mx_operand("h%d%d" % (part, half), HALF) for part in range(2) for half in range(2)}
+        q_f32 = {(part, tile): kept("q%d%d" % (part, tile), [P, TILE, PACK], F32)
+                 for part in range(2) for tile in range(S // TILE)}
+        banks = [psum.tile([P, BANK], F32, name="bank%d" % i) for i in range(8)]
+
+        x_planes = xT.rearrange("(a p t) j -> a t p j", a=2, t=PACK)
+        out_rows = out.rearrange("(s p) j -> p s j", p=P)
         x_sb = {}
-        w_raw = {}
-        count = {"w": 0, "x": 0, "h": 0, "q": 0, "e": 0}
+        w_f32 = {}
+        w_mx = {}
+        w_staged = []
 
-        def nxt(key):
-            count[key] = count[key] + 1
-            return count[key] - 1
+        def load_plane(plane):
+            x_sb[plane] = x_pool.tile([P, T2], F32, name="x_plane", align_bytes=DMA_ALIGN)
+            nc.sync.dma_start(out=x_sb[plane][:], in_=x_planes[plane // PACK, plane % PACK])
 
-        x_planes = xT.rearrange("(a p i) t -> a i p t", a=2, i=4)
+        def load_weight(piece, weight, a, column_block):
+            rows = weight[PASS * a:PASS * (a + 1), PASS * column_block:PASS * (column_block + 1)]
+            w_f32[piece] = w_pool.tile([P, PACK, PASS], F32, name="w_f32", align_bytes=DMA_ALIGN)
+            nc.sync.dma_start(out=w_f32[piece][:], in_=rows.rearrange("(p t) c -> p t c", t=PACK))
 
-        def load_x(pl):
-            x_sb[pl] = xpool.tile([P, T2], F32, name="x_plane")
-            nc.sync.dma_start(out=x_sb[pl][:], in_=x_planes[pl // 4, pl % 4])
+        def quantize(operand, columns, stage):
+            nc.vector.quantize_mx(out=operand[0][:, columns].bitcast(FP8X4), scales=operand[1][:, columns], in_=stage)
 
-        def load_w(name, src, a, c):
-            w_raw[name] = wpool.tile([P, 4, 512], F32, name="w_raw")
-            nc.sync.dma_start(out=w_raw[name][:],
-                              in_=src[512 * a:512 * (a + 1), 512 * c:512 * (c + 1)].rearrange("(p j) c -> p j c", j=4))
-
-        def quantize(dst, cols, src):
-            nc.vector.quantize_mx(out=dst[0][:, cols].bitcast(FP8), scales=dst[1][:, cols], in_=src)
-
-        def prep_w(name, permute):
-            st = w_stage[nxt("w") % 2]
-            raw = w_raw[name]
-            if permute:
-                nc.scalar.copy(out=st[:].rearrange("p (u v m j) -> p u m j v", u=2, v=2, j=4),
-                               in_=raw[:].rearrange("p j (m u v) -> p u m j v", u=2, v=2))
+        def interleave_weight(piece, feeds_h):
+            stage = w_stage[len(w_staged) % 2]
+            w_staged.append(piece)
+            if feeds_h:
+                nc.scalar.copy(out=stage[:].rearrange("p (u v m t) -> p u m t v", u=2, v=2, t=PACK),
+                               in_=w_f32[piece][:].rearrange("p t (m u v) -> p u m t v", u=2, v=2))
             else:
-                nc.scalar.copy(out=st[:].rearrange("p (c i j) -> p c j i", i=4, j=4),
-                               in_=raw[:].rearrange("p j (c i) -> p c j i", i=4))
-            wq[name] = (kept(name + "_w", [P, 512], U32), kept(name + "_s", [P, 512], U8))
-            quantize(wq[name], slice(0, 512), st[:])
+                nc.scalar.copy(out=stage[:].rearrange("p (c i t) -> p c t i", i=4, t=PACK),
+                               in_=w_f32[piece][:].rearrange("p t (c i) -> p c t i", i=4))
+            w_mx[piece] = mx_operand(piece, PASS)
 
-        def gather_x(pl, j0, j1):
-            win = x_sb[pl][:].indirect(head_lists[:, j0 // 16:j1 // 16])
-            dst = picked[pl // 4][:, pl % 4, j0:j1]
-            if MODE == "C":
-                nc.vector.tensor_tensor(dst, win, wgt_sb[:, j0:j1], MULT)
-            else:
-                nc.vector.tensor_copy(dst, win)
+        def quantize_weight(piece):
+            quantize(w_mx[piece], slice(0, PASS), w_stage[w_staged.index(piece) % 2][:])
 
-        def weigh(a, q):
-            st = x_stage[nxt("x") % 2]
-            cols = slice(256 * q, 256 * (q + 1))
-            src = picked[a][:, :, cols].rearrange("p t (c i) -> p c t i", i=4)
-            dst = st[:].rearrange("p (c i t) -> p c t i", i=4, t=4)
-            if MODE == "C":
-                nc.scalar.copy(out=dst, in_=src)
-            else:
-                w_b = wgt_sb[:, cols].rearrange("p (c i) -> p c i", i=4).unsqueeze(2).to_broadcast([P, 64, 4, 4])
-                nc.vector.tensor_tensor(dst, src, w_b, MULT)
-            return lambda: quantize(xq[a, q // 2], slice(256 * (q % 2), 256 * (q % 2 + 1)), st[:])
+        def gather_plane(plane, j0, j1):
+            window = x_sb[plane][:].indirect(head_lists[:, j0 // LIST_ROWS:j1 // LIST_ROWS])
+            nc.vector.tensor_tensor(xg_f32[plane // PACK][:, plane % PACK, j0:j1], window, wgt_sb[:, j0:j1], MULT)
 
-        def mm(dst, lhs, lcols, rhs, rcols, start, stop):
-            nc.tensor.matmul_mx(out=dst, lhsT=lhs[0][:, lcols].bitcast(FP8), lhsT_scale=lhs[1][:, lcols],
-                                rhs=rhs[0][:, rcols].bitcast(FP8), rhs_scale=rhs[1][:, rcols], start=start, stop=stop)
+        def interleave_xg(a, quarter):
+            source = xg_f32[a][:, :, QUARTER * quarter:QUARTER * (quarter + 1)]
+            nc.scalar.copy(out=xg_stage[quarter % 2][:].rearrange("p (c i t) -> p c t i", i=4, t=PACK),
+                           in_=source.rearrange("p t (c i) -> p c t i", i=4))
 
-        def relation(c, tt):
-            bank = banks[nxt("q") % 8]
-            for t in range(4):
-                mm(bank[:, 128 * t:128 * (t + 1)], wq["wr%d" % c], slice(128 * t, 128 * (t + 1)),
-                   (v_w, v_s), slice(128 * tt, 128 * (tt + 1)), True, True)
-            nc.scalar.copy(out=q_sb[c, tt][:], in_=bank[:].rearrange("p (t n) -> p n t", t=4))
+        def quantize_xg(a, quarter):
+            j0 = QUARTER * (quarter % 2)
+            quantize(xg_mx[a, quarter // 2], slice(j0, j0 + QUARTER), xg_stage[quarter % 2][:])
 
-        def entity(c, q):
-            st = h_stage[nxt("h") % 2]
-            for u in range(2):
-                tt = 2 * q + u
-                bank = banks[nxt("e") % 4]
-                rc = slice(128 * (tt % 4), 128 * (tt % 4 + 1))
-                for t in range(4):
-                    for a in range(2):
-                        mm(bank[:, 128 * t:128 * (t + 1)], wq["we%d%d" % (a, c)], slice(128 * t, 128 * (t + 1)),
-                           xq[a, tt // 4], rc, a == 0, a == 1)
-                nc.vector.tensor_tensor(st[:, 512 * u:512 * (u + 1)].rearrange("p (n t) -> p n t", t=4),
-                                        bank[:].rearrange("p (t n) -> p n t", t=4), q_sb[c, tt][:], MULT)
-            return lambda: quantize(hq[c, q // 2], slice(256 * (q % 2), 256 * (q % 2 + 1)), st[:])
+        def quantize_h(part, half, j0, j1):
+            quantize(h_mx[part, half], slice(j0, j1), h_stage[part][:, PACK * j0:PACK * j1])
 
-        def z_dst(j0, width, bank0, nt):
-            per = 512 // width
-            return banks[bank0 + nt // per][:, width * (nt % per):width * (nt % per + 1)]
+        def matmul_e4m3(psum_out, stationary, m_columns, moving, n_columns, start, stop):
+            nc.tensor.matmul_mx(out=psum_out,
+                                lhsT=stationary[0][:, m_columns].bitcast(FP8X4), lhsT_scale=stationary[1][:, m_columns],
+                                rhs=moving[0][:, n_columns].bitcast(FP8X4), rhs_scale=moving[1][:, n_columns],
+                                start=start, stop=stop)
 
-        def score_head(j0, width, bank0, a):
-            per = 512 // width
-            for nt in range(4):
-                mm(z_dst(j0, width, bank0, nt), wq["wp%d" % a], slice(128 * nt, 128 * (nt + 1)),
-                   xq[a, j0 // 512], slice(j0 % 512, j0 % 512 + width), a == 0 and nt % per == 0, False)
+        def project_relations(part, tile):
+            bank = banks[tile]
+            for s in range(PACK):
+                matmul_e4m3(bank[:, TILE * s:TILE * (s + 1)], w_mx["wr%d" % part], slice(P * s, P * (s + 1)),
+                            v_mx, slice(TILE * tile, TILE * (tile + 1)), True, True)
+            nc.scalar.copy(out=q_f32[part, tile][:], in_=bank[:].rearrange("p (s j) -> p j s", s=PACK))
 
-        def score_tail(j0, width, bank0, c, nts):
-            per = 512 // width
-            step = 512 if width == 512 else 128
-            for nt in nts:
-                for s0 in range(0, width, step):
-                    rc = slice(j0 % 512 + s0, j0 % 512 + s0 + step)
-                    nc.tensor.matmul_mx(
-                        out=z_dst(j0, width, bank0, nt)[:, s0:s0 + step],
-                        lhsT=w4_w[:, c, 256 * nt:256 * (nt + 1)].bitcast(FP4),
-                        lhsT_scale=w4_s[:, c, 128 * nt:128 * (nt + 1)],
-                        rhs=hq[c, j0 // 512][0][:, rc].bitcast(FP8), rhs_scale=hq[c, j0 // 512][1][:, rc],
-                        start=False, stop=(c == 1 and nt % per == per - 1 and s0 + step == width))
+        def e_bank(part, tile):
+            return banks[tile % 4 + (4 if part == 1 and tile < 4 else 0)]
 
-        out_v = out.rearrange("(c p) j -> p c j", p=P)
+        def project_entities(part, tile, a):
+            j0 = TILE * (tile % 4)
+            for s in range(PACK):
+                matmul_e4m3(e_bank(part, tile)[:, TILE * s:TILE * (s + 1)],
+                            w_mx["we%d%d" % (a, part)], slice(P * s, P * (s + 1)),
+                            xg_mx[a, tile // 4], slice(j0, j0 + TILE), a == 0 and s == 0, a == 1 and s == PACK - 1)
 
-        def finish(j0, width, bank0):
-            per = 512 // width
-            res = wpool.tile([P, 4, width], F32, name="w_raw")
-            for n0 in range(0, 4, 2):
-                score_tail(j0, width, bank0, 1, range(n0, n0 + 2))
-                for nt in range(n0, n0 + 2):
-                    nc.scalar.activation(out=res[:, nt, :], in_=z_dst(j0, width, bank0, nt), func=SIGMOID,
-                                         bias=bias[:, nt:nt + 1])
-                nc.sync.dma_start(out=out_v[:, n0:n0 + 2, j0:j0 + width], in_=res[:, n0:n0 + 2, :])
+        def make_h(part, tile):
+            project_entities(part, tile, 1)
+            j0 = TILE * (tile % 4)
+            nc.vector.tensor_tensor(h_stage[part][:, PACK * j0:PACK * (j0 + TILE)].rearrange("p (j s) -> p j s", s=PACK),
+                                    e_bank(part, tile)[:].rearrange("p (s j) -> p j s", s=PACK),
+                                    q_f32[part, tile][:], MULT)
 
-        nc.gpsimd.memset(tab_s[:].bitcast(I32), 0)
-        nc.gpsimd.memset(w4_s[:].bitcast(I32), 0)
+        def score_head(half, s, a, start=False, stop=False):
+            matmul_e4m3(banks[4 + s][:], w_mx["wp%d" % a], slice(P * s, P * (s + 1)),
+                        xg_mx[a, half], slice(0, HALF), start, stop)
 
-        nc.sync.dma_start(rel_list[:], offs)
-        nc.sync.dma_start(out=tab_w[:], in_=tab_words[0].rearrange("p t i -> p (t i)").bitcast(I32))
+        def score_triple(half, s, part, start=False, stop=False):
+            nc.tensor.matmul_mx(out=banks[4 + s][:],
+                                lhsT=w4_words_sb[:, part, 2 * P * s:2 * P * (s + 1)].bitcast(FP4X4),
+                                lhsT_scale=w4_scales_sb[:, part, P * s:P * (s + 1)],
+                                rhs=h_mx[part, half][0][:].bitcast(FP8X4), rhs_scale=h_mx[part, half][1][:],
+                                start=start, stop=stop)
+
+        def sigmoid(result, s, j0, j1):
+            nc.scalar.activation(out=result[:, s, j0:j1], in_=banks[4 + s][:, j0:j1], func=SIGMOID, bias=bias[:, s:s + 1])
+
+        nc.gpsimd.memset(table_scales[:].bitcast(I32), 0)
+        nc.gpsimd.memset(w4_scales_sb[:].bitcast(I32), 0)
+        for quadrant in range(4):
+            nc.gpsimd.dma_start(
+                out=w4_scales_sb[32 * quadrant:32 * quadrant + 4, :, :].bitcast(I32),
+                in_=w4_scales[:, 4 * quadrant:4 * quadrant + 4, :].rearrange("a r n -> r a n").bitcast(I32))
+
+        nc.sync.dma_start(relation_list[:], offs)
+        nc.sync.dma_start(out=table_words[:], in_=tab_words[0].rearrange("p j t -> p (j t)").bitcast(I32))
+        load_weight("wr0", wr, 0, 0)
+        for quadrant in range(4):
+            nc.sync.dma_start(out=table_scales[32 * quadrant:32 * quadrant + 4, :].bitcast(I32),
+                              in_=tab_scales[0, 4 * quadrant:4 * quadrant + 4, :].bitcast(I32))
         nc.sync.dma_start(head_lists[:], offs2)
-
-        load_x(0)
-        for qd in range(4):
-            nc.sync.dma_start(out=tab_s[32 * qd:32 * qd + 4, :].bitcast(I32),
-                              in_=tab_scales[0, 4 * qd:4 * qd + 4, :].bitcast(I32))
-        load_w("wr0", wr, 0, 0)
-        load_x(1)
-        load_x(2)
-        load_x(3)
+        load_weight("wr1", wr, 0, 1)
         nc.sync.dma_start(out=wgt_sb[:], in_=wgt)
-        load_w("wr1", wr, 0, 1)
-        load_x(4)
-        load_w("we00", we, 0, 0)
-        load_x(5)
+        for plane in range(5):
+            load_plane(plane)
+        load_weight("we00", we, 0, 0)
+        load_plane(5)
+        load_plane(6)
 
-        nc.vector.tensor_copy(v_w[:], tab_w[:].bitcast(U32).indirect(rel_list[:]))
-        gather_x(0, 0, S)
-        load_x(6)
-        nc.vector.tensor_copy(v_s[:], tab_s[:].indirect(rel_list[:]))
-        prep_w("wr0", True)
-        load_w("we10", we, 1, 0)
-        gather_x(1, 0, S)
-        load_x(7)
-        load_w("we01", we, 0, 1)
-        for tt in range(8):
-            relation(0, tt)
-        gather_x(2, 0, S)
-        gather_x(3, 0, S)
-        prep_w("wr1", True)
-        load_w("we11", we, 1, 1)
-        nc.sync.dma_start(out=w4_w[:].bitcast(I32), in_=w4_words.rearrange("a p c -> p a c").bitcast(I32))
-        for qd in range(4):
-            nc.sync.dma_start(out=w4_s[32 * qd:32 * qd + 4, :, :].bitcast(I32),
-                              in_=w4_scales[:, 4 * qd:4 * qd + 4, :].rearrange("a r n -> r a n").bitcast(I32))
-        with nc.allow_non_contiguous_dma(reason="one bias value a partition"):
-            nc.sync.dma_start(out=bias[:], in_=b.rearrange("(c p) -> p c", p=P))
-        q0 = weigh(0, 0)
-        q1 = weigh(0, 1)
-        q0()
-        q1()
-        for tt in range(8):
-            relation(1, tt)
-        gather_x(4, 0, S)
-        prep_w("we00", True)
-        load_w("wp0", wp, 0, 0)
-        gather_x(5, 0, S)
-        gather_x(6, 0, S)
-        prep_w("we10", True)
-        load_w("wp1", wp, 1, 0)
-        gather_x(7, 0, 512)
-        q0 = weigh(1, 0)
-        q1 = weigh(1, 1)
-        q0()
-        gather_x(7, 512, S)
-        q1()
-        prep_w("we01", True)
-        h0 = entity(0, 0)
-        q0 = weigh(0, 2)
-        h0()
-        h1 = entity(0, 1)
-        q0()
-        prep_w("we11", True)
-        q1 = weigh(1, 2)
-        h1()
-        q0 = weigh(0, 3)
-        q1()
-        h0 = entity(1, 0)
-        q0()
-        prep_w("wp0", False)
-        q1 = weigh(1, 3)
-        h0()
-        h1 = entity(1, 1)
-        q1()
-        prep_w("wp1", False)
-        h0 = entity(0, 2)
-        h1()
-        score_head(0, 512, 4, 0)
-        score_head(0, 512, 4, 1)
-        score_tail(0, 512, 4, 0, range(4))
-        h1 = entity(1, 2)
-        h0()
-        finish(0, 512, 4)
-        h0 = entity(0, 3)
-        h1()
-        score_head(512, 256, 4, 0)
-        score_head(512, 256, 4, 1)
-        score_tail(512, 256, 4, 0, range(4))
-        h1 = entity(1, 3)
-        h0()
-        finish(512, 256, 4)
-        score_head(768, 256, 6, 0)
-        score_head(768, 256, 6, 1)
-        score_tail(768, 256, 6, 0, range(4))
-        h1()
-        finish(768, 256, 6)
+        nc.vector.tensor_copy(v_mx[0][:], table_words[:].bitcast(U32).indirect(relation_list[:]))
+        nc.vector.tensor_copy(v_mx[1][:], table_scales[:].indirect(relation_list[:]))
+        for piece in ("wr0", "wr1"):
+            interleave_weight(piece, True)
+            quantize_weight(piece)
+
+        gather_plane(0, 0, S)
+        load_weight("we10", we, 1, 0)
+        load_plane(7)
+        load_weight("we01", we, 0, 1)
+        for tile in range(S // TILE):
+            project_relations(0, tile)
+        gather_plane(1, 0, S)
+        load_weight("we11", we, 1, 1)
+        nc.sync.dma_start(out=w4_words_sb[:].bitcast(I32), in_=w4_words.rearrange("a p c -> p a c").bitcast(I32))
+        with nc.allow_non_contiguous_dma(reason="one bias value for each partition and bank of tails"):
+            nc.sync.dma_start(out=bias[:], in_=b.rearrange("(s p) -> p s", p=P))
+        gather_plane(2, 0, S)
+        gather_plane(3, 0, S)
+        for tile in range(S // TILE):
+            project_relations(1, tile)
+
+        gather_plane(4, 0, S)
+        interleave_xg(0, 0)
+        interleave_xg(0, 1)
+        gather_plane(5, 0, S)
+        quantize_xg(0, 0)
+        quantize_xg(0, 1)
+        interleave_weight("we00", True)
+        load_weight("wp0", wp, 0, 0)
+        interleave_xg(0, 2)
+        interleave_xg(0, 3)
+        gather_plane(6, 0, S)
+        quantize_weight("we00")
+        quantize_xg(0, 2)
+        quantize_xg(0, 3)
+        for tile in range(4):
+            project_entities(0, tile, 0)
+        interleave_weight("we10", True)
+        quantize_weight("we10")
+
+        for quarter in range(2):
+            gather_plane(7, QUARTER * quarter, QUARTER * (quarter + 1))
+            interleave_xg(1, quarter)
+        gather_plane(7, HALF, S)
+        quantize_xg(1, 0)
+        load_weight("wp1", wp, 1, 0)
+        quantize_xg(1, 1)
+
+        interleave_weight("we01", True)
+        make_h(0, 0)
+        make_h(0, 1)
+        quantize_weight("we01")
+        interleave_weight("we11", True)
+        make_h(0, 2)
+        make_h(0, 3)
+        for tile in range(4):
+            project_entities(1, tile, 0)
+        for tile in range(4, 8):
+            project_entities(0, tile, 0)
+        quantize_weight("we11")
+        quantize_h(0, 0, 0, HALF)
+        interleave_xg(1, 2)
+        interleave_xg(1, 3)
+        make_h(1, 0)
+        quantize_xg(1, 2)
+        make_h(1, 1)
+        quantize_xg(1, 3)
+        interleave_weight("wp0", False)
+        make_h(1, 2)
+        make_h(1, 3)
+        make_h(0, 4)
+        quantize_h(1, 0, 0, HALF)
+        quantize_weight("wp0")
+        interleave_weight("wp1", False)
+        make_h(0, 5)
+        make_h(0, 6)
+        quantize_weight("wp1")
+        make_h(0, 7)
+        for tile in range(4, 8):
+            project_entities(1, tile, 0)
+            make_h(1, tile)
+            if tile == 4:
+                quantize_h(0, 1, 0, HALF)
+            if tile >= 6:
+                quantize_h(1, 1, QUARTER * (tile - 6), QUARTER * (tile - 5))
+
+        for part in range(2):
+            for s in range(N // P):
+                score_triple(0, s, part, start=(part == 0))
+        result = w_pool.tile([P, N // P, HALF], F32, name="w_f32", align_bytes=DMA_ALIGN)
+        for s in range(N // P):
+            score_head(0, s, 0)
+            score_head(0, s, 1, stop=True)
+            sigmoid(result, s, 0, HALF)
+            if s % 2 == 1:
+                nc.sync.dma_start(out=out_rows[:, s - 1:s + 1, 0:HALF], in_=result[:, s - 1:s + 1, :])
+
+        for s in range(N // P):
+            score_head(1, s, 0, start=True)
+        result = w_pool.tile([P, N // P, HALF], F32, name="w_f32", align_bytes=DMA_ALIGN)
+        for s in range(N // P):
+            score_head(1, s, 1)
+            score_triple(1, s, 0)
+            score_triple(1, s, 1, stop=True)
+            if s < N // P - 1:
+                sigmoid(result, s, 0, HALF)
+                nc.sync.dma_start(out=out_rows[:, s:s + 1, HALF:S], in_=result[:, s:s + 1, :])
+            else:
+                for j0, queue in ((0, nc.sync), (QUARTER, nc.scalar)):
+                    sigmoid(result, s, j0, j0 + QUARTER)
+                    queue.dma_start(out=out_rows[:, s, HALF + j0:HALF + j0 + QUARTER], in_=result[:, s, j0:j0 + QUARTER])

@@ -26,6 +26,8 @@ MX_ALIGN = 64
 DMA_ALIGN = 256
 X_BUFS = 7
 W_BUFS = 4
+GROUPS = PASS // PACK
+GROUPS_ON_VECTOR = {"wr1": GROUPS, "we01": GROUPS // 2}
 
 
 def tile_list_triple_tail_score_kernel(tc, xT, wgt, offs2, tab_words, tab_scales, offs,
@@ -85,8 +87,13 @@ def tile_list_triple_tail_score_kernel(tc, xT, wgt, offs2, tab_words, tab_scales
             stage = w_stage[len(w_staged) % 2]
             w_staged.append(piece)
             if feeds_h:
-                nc.scalar.copy(out=stage[:].rearrange("p (u v m t) -> p u m t v", u=2, v=2, t=PACK),
-                               in_=w_f32[piece][:].rearrange("p t (m u v) -> p u m t v", u=2, v=2))
+                target = stage[:].rearrange("p (u v m t) -> p u m t v", u=2, v=2, t=PACK)
+                source = w_f32[piece][:].rearrange("p t (m u v) -> p u m t v", u=2, v=2)
+                cut = GROUPS - GROUPS_ON_VECTOR.get(piece, 0)
+                if cut > 0:
+                    nc.scalar.copy(out=target[:, :, 0:cut, :, :], in_=source[:, :, 0:cut, :, :])
+                if cut < GROUPS:
+                    nc.vector.tensor_copy(out=target[:, :, cut:GROUPS, :, :], in_=source[:, :, cut:GROUPS, :, :])
             else:
                 nc.scalar.copy(out=stage[:].rearrange("p (c i t) -> p c t i", i=4, t=PACK),
                                in_=w_f32[piece][:].rearrange("p t (c i) -> p c t i", i=4))
@@ -169,9 +176,11 @@ def tile_list_triple_tail_score_kernel(tc, xT, wgt, offs2, tab_words, tab_scales
             nc.sync.dma_start(out=table_scales[32 * quadrant:32 * quadrant + 4, :].bitcast(I32),
                               in_=tab_scales[0, 4 * quadrant:4 * quadrant + 4, :].bitcast(I32))
         nc.sync.dma_start(head_lists[:], offs2)
-        load_weight("wr1", wr, 0, 1)
         nc.sync.dma_start(out=wgt_sb[:], in_=wgt)
-        for plane in range(5):
+        load_plane(0)
+        load_plane(1)
+        load_weight("wr1", wr, 0, 1)
+        for plane in range(2, 5):
             load_plane(plane)
         load_weight("we00", we, 0, 0)
         load_plane(5)
@@ -179,9 +188,8 @@ def tile_list_triple_tail_score_kernel(tc, xT, wgt, offs2, tab_words, tab_scales
 
         nc.vector.tensor_copy(v_mx[0][:], table_words[:].bitcast(U32).indirect(relation_list[:]))
         nc.vector.tensor_copy(v_mx[1][:], table_scales[:].indirect(relation_list[:]))
-        for piece in ("wr0", "wr1"):
-            interleave_weight(piece, True)
-            quantize_weight(piece)
+        interleave_weight("wr0", True)
+        quantize_weight("wr0")
 
         gather_plane(0, 0, S)
         load_weight("we10", we, 1, 0)
@@ -190,6 +198,8 @@ def tile_list_triple_tail_score_kernel(tc, xT, wgt, offs2, tab_words, tab_scales
         for tile in range(S // TILE):
             project_relations(0, tile)
         gather_plane(1, 0, S)
+        interleave_weight("wr1", True)
+        quantize_weight("wr1")
         load_weight("we11", we, 1, 1)
         nc.sync.dma_start(out=w4_words_sb[:].bitcast(I32), in_=w4_words.rearrange("a p c -> p a c").bitcast(I32))
         with nc.allow_non_contiguous_dma(reason="one bias value for each partition and bank of tails"):
@@ -222,14 +232,14 @@ def tile_list_triple_tail_score_kernel(tc, xT, wgt, offs2, tab_words, tab_scales
             gather_plane(7, QUARTER * quarter, QUARTER * (quarter + 1))
             interleave_xg(1, quarter)
         gather_plane(7, HALF, S)
+        interleave_weight("we01", True)
         quantize_xg(1, 0)
         load_weight("wp1", wp, 1, 0)
         quantize_xg(1, 1)
+        quantize_weight("we01")
 
-        interleave_weight("we01", True)
         make_h(0, 0)
         make_h(0, 1)
-        quantize_weight("we01")
         interleave_weight("we11", True)
         make_h(0, 2)
         make_h(0, 3)

from contextlib import ExitStack

import concourse.mybir as mybir

K, D, T2, T, S, H, N = 1024, 512, 2048, 2048, 1024, 1024, 512
FLOPS = 2 * S * (K * H + D * H + H * N + K * N)

F32 = mybir.dt.float32
BF16 = mybir.dt.bfloat16
I32 = mybir.dt.int32
U32 = mybir.dt.uint32
U16 = mybir.dt.uint16
U8 = mybir.dt.uint8
FP8X4 = mybir.dt.float8_e4m3fn_x4
FP4X4 = mybir.dt.float4_e2m1fn_x4
MULT = mybir.AluOpType.mult
SIGMOID = mybir.ActivationFunctionType.Sigmoid

P = 128
PACK = 4
PASS = P * PACK
BANK = 512
TILE, QUARTER, HALF = 128, 256, 512
LIST_ROWS = 16
MX_ALIGN = 64
DMA_ALIGN = 256
X_BUFS = 7
W_BUFS = 4
GROUPS = PASS // PACK
GROUPS_ON_VECTOR = {"wr1": GROUPS, "we01": GROUPS // 2}


def tile_list_triple_tail_score_kernel(tc, xT, wgt, offs2, tab_words, tab_scales, offs,
                                                 we, wr, wp, w4_words, w4_scales, b, out):
    nc = tc.nc
    with ExitStack() as ctx:
        keep = ctx.enter_context(tc.tile_pool(name="keep", bufs=1))
        x_pool = ctx.enter_context(tc.tile_pool(name="x_pool", bufs=X_BUFS))
        w_pool = ctx.enter_context(tc.tile_pool(name="w_pool", bufs=W_BUFS))
        psum = ctx.enter_context(tc.psum_pool(name="psum", bufs=1))

        def kept(name, shape, dtype, align=MX_ALIGN):
            return keep.tile(shape, dtype, name=name, align_bytes=align)

        def mx_operand(name, columns):
            return kept(name + "_words", [P, columns], U32), kept(name + "_scales", [P, columns], U8)

        relation_list = keep.tile([P, S // LIST_ROWS], U16, name="relation_list")
        head_lists = keep.tile([P, S // LIST_ROWS], U16, name="head_lists")
        table_words = kept("table_words", [P, T], I32, DMA_ALIGN)
        table_scales = kept("table_scales", [P, T], U8)
        v_mx = mx_operand("v", S)
        wgt_sb = kept("wgt_sb", [P, S], F32, DMA_ALIGN)
        w4_words_sb = kept("w4_words_sb", [P, 2, 2 * N], U8)
        w4_scales_sb = kept("w4_scales_sb", [P, 2, N], U8)
        bias = kept("bias", [P, N // P], F32)
        xg_f32 = [kept("xg_f32_%d" % a, [P, PACK, S], F32) for a in range(2)]
        xg_stage = [kept("xg_stage%d" % i, [P, PACK * QUARTER], BF16) for i in range(2)]
        w_stage = [kept("w_stage%d" % i, [P, PACK * PASS], BF16) for i in range(2)]
        h_stage = [kept("h_stage%d" % part, [P, PACK * HALF], BF16) for part in range(2)]
        xg_mx = {(a, half): mx_operand("xg%d%d" % (a, half), HALF) for a in range(2) for half in range(2)}
        h_mx = {(part, half): mx_operand("h%d%d" % (part, half), HALF) for part in range(2) for half in range(2)}
        q_f32 = {(part, tile): kept("q%d%d" % (part, tile), [P, TILE, PACK], F32)
                 for part in range(2) for tile in range(S // TILE)}
        banks = [psum.tile([P, BANK], F32, name="bank%d" % i) for i in range(8)]

        x_planes = xT.rearrange("(a p t) j -> a t p j", a=2, t=PACK)
        out_rows = out.rearrange("(s p) j -> p s j", p=P)
        x_sb = {}
        w_f32 = {}
        w_mx = {}
        w_staged = []

        def load_plane(plane):
            x_sb[plane] = x_pool.tile([P, T2], F32, name="x_plane", align_bytes=DMA_ALIGN)
            nc.sync.dma_start(out=x_sb[plane][:], in_=x_planes[plane // PACK, plane % PACK])

        def load_weight(piece, weight, a, column_block):
            rows = weight[PASS * a:PASS * (a + 1), PASS * column_block:PASS * (column_block + 1)]
            w_f32[piece] = w_pool.tile([P, PACK, PASS], F32, name="w_f32", align_bytes=DMA_ALIGN)
            nc.sync.dma_start(out=w_f32[piece][:], in_=rows.rearrange("(p t) c -> p t c", t=PACK))

        def quantize(operand, columns, stage):
            nc.vector.quantize_mx(out=operand[0][:, columns].bitcast(FP8X4), scales=operand[1][:, columns], in_=stage)

        def interleave_weight(piece, feeds_h):
            stage = w_stage[len(w_staged) % 2]
            w_staged.append(piece)
            if feeds_h:
                target = stage[:].rearrange("p (u v m t) -> p u m t v", u=2, v=2, t=PACK)
                source = w_f32[piece][:].rearrange("p t (m u v) -> p u m t v", u=2, v=2)
                cut = GROUPS - GROUPS_ON_VECTOR.get(piece, 0)
                if cut > 0:
                    nc.scalar.copy(out=target[:, :, 0:cut, :, :], in_=source[:, :, 0:cut, :, :])
                if cut < GROUPS:
                    nc.vector.tensor_copy(out=target[:, :, cut:GROUPS, :, :], in_=source[:, :, cut:GROUPS, :, :])
            else:
                nc.scalar.copy(out=stage[:].rearrange("p (c i t) -> p c t i", i=4, t=PACK),
                               in_=w_f32[piece][:].rearrange("p t (c i) -> p c t i", i=4))
            w_mx[piece] = mx_operand(piece, PASS)

        def quantize_weight(piece):
            quantize(w_mx[piece], slice(0, PASS), w_stage[w_staged.index(piece) % 2][:])

        def gather_plane(plane, j0, j1):
            window = x_sb[plane][:].indirect(head_lists[:, j0 // LIST_ROWS:j1 // LIST_ROWS])
            nc.vector.tensor_tensor(xg_f32[plane // PACK][:, plane % PACK, j0:j1], window, wgt_sb[:, j0:j1], MULT)

        def interleave_xg(a, quarter):
            source = xg_f32[a][:, :, QUARTER * quarter:QUARTER * (quarter + 1)]
            nc.scalar.copy(out=xg_stage[quarter % 2][:].rearrange("p (c i t) -> p c t i", i=4, t=PACK),
                           in_=source.rearrange("p t (c i) -> p c t i", i=4))

        def quantize_xg(a, quarter):
            j0 = QUARTER * (quarter % 2)
            quantize(xg_mx[a, quarter // 2], slice(j0, j0 + QUARTER), xg_stage[quarter % 2][:])

        def quantize_h(part, half, j0, j1):
            quantize(h_mx[part, half], slice(j0, j1), h_stage[part][:, PACK * j0:PACK * j1])

        def matmul_e4m3(psum_out, stationary, m_columns, moving, n_columns, start, stop):
            nc.tensor.matmul_mx(out=psum_out,
                                lhsT=stationary[0][:, m_columns].bitcast(FP8X4), lhsT_scale=stationary[1][:, m_columns],
                                rhs=moving[0][:, n_columns].bitcast(FP8X4), rhs_scale=moving[1][:, n_columns],
                                start=start, stop=stop)

        def project_relations(part, tile):
            bank = banks[tile]
            for s in range(PACK):
                matmul_e4m3(bank[:, TILE * s:TILE * (s + 1)], w_mx["wr%d" % part], slice(P * s, P * (s + 1)),
                            v_mx, slice(TILE * tile, TILE * (tile + 1)), True, True)
            nc.scalar.copy(out=q_f32[part, tile][:], in_=bank[:].rearrange("p (s j) -> p j s", s=PACK))

        def e_bank(part, tile):
            return banks[tile % 4 + (4 if part == 1 and tile < 4 else 0)]

        def project_entities(part, tile, a):
            j0 = TILE * (tile % 4)
            for s in range(PACK):
                matmul_e4m3(e_bank(part, tile)[:, TILE * s:TILE * (s + 1)],
                            w_mx["we%d%d" % (a, part)], slice(P * s, P * (s + 1)),
                            xg_mx[a, tile // 4], slice(j0, j0 + TILE), a == 0 and s == 0, a == 1 and s == PACK - 1)

        def make_h(part, tile):
            project_entities(part, tile, 1)
            j0 = TILE * (tile % 4)
            nc.vector.tensor_tensor(h_stage[part][:, PACK * j0:PACK * (j0 + TILE)].rearrange("p (j s) -> p j s", s=PACK),
                                    e_bank(part, tile)[:].rearrange("p (s j) -> p j s", s=PACK),
                                    q_f32[part, tile][:], MULT)

        def score_head(half, s, a, start=False, stop=False):
            matmul_e4m3(banks[4 + s][:], w_mx["wp%d" % a], slice(P * s, P * (s + 1)),
                        xg_mx[a, half], slice(0, HALF), start, stop)

        def score_triple(half, s, part, start=False, stop=False):
            nc.tensor.matmul_mx(out=banks[4 + s][:],
                                lhsT=w4_words_sb[:, part, 2 * P * s:2 * P * (s + 1)].bitcast(FP4X4),
                                lhsT_scale=w4_scales_sb[:, part, P * s:P * (s + 1)],
                                rhs=h_mx[part, half][0][:].bitcast(FP8X4), rhs_scale=h_mx[part, half][1][:],
                                start=start, stop=stop)

        def sigmoid(result, s, j0, j1):
            nc.scalar.activation(out=result[:, s, j0:j1], in_=banks[4 + s][:, j0:j1], func=SIGMOID, bias=bias[:, s:s + 1])

        nc.gpsimd.memset(table_scales[:].bitcast(I32), 0)
        nc.gpsimd.memset(w4_scales_sb[:].bitcast(I32), 0)
        for quadrant in range(4):
            nc.gpsimd.dma_start(
                out=w4_scales_sb[32 * quadrant:32 * quadrant + 4, :, :].bitcast(I32),
                in_=w4_scales[:, 4 * quadrant:4 * quadrant + 4, :].rearrange("a r n -> r a n").bitcast(I32))

        nc.sync.dma_start(relation_list[:], offs)
        nc.sync.dma_start(out=table_words[:], in_=tab_words[0].rearrange("p j t -> p (j t)").bitcast(I32))
        load_weight("wr0", wr, 0, 0)
        for quadrant in range(4):
            nc.sync.dma_start(out=table_scales[32 * quadrant:32 * quadrant + 4, :].bitcast(I32),
                              in_=tab_scales[0, 4 * quadrant:4 * quadrant + 4, :].bitcast(I32))
        nc.sync.dma_start(head_lists[:], offs2)
        nc.sync.dma_start(out=wgt_sb[:], in_=wgt)
        load_plane(0)
        load_plane(1)
        load_weight("wr1", wr, 0, 1)
        for plane in range(2, 5):
            load_plane(plane)
        load_weight("we00", we, 0, 0)
        load_plane(5)
        load_plane(6)

        nc.vector.tensor_copy(v_mx[0][:], table_words[:].bitcast(U32).indirect(relation_list[:]))
        nc.vector.tensor_copy(v_mx[1][:], table_scales[:].indirect(relation_list[:]))
        interleave_weight("wr0", True)
        quantize_weight("wr0")

        gather_plane(0, 0, S)
        load_weight("we10", we, 1, 0)
        load_plane(7)
        load_weight("we01", we, 0, 1)
        for tile in range(S // TILE):
            project_relations(0, tile)
        gather_plane(1, 0, S)
        interleave_weight("wr1", True)
        quantize_weight("wr1")
        load_weight("we11", we, 1, 1)
        nc.sync.dma_start(out=w4_words_sb[:].bitcast(I32), in_=w4_words.rearrange("a p c -> p a c").bitcast(I32))
        with nc.allow_non_contiguous_dma(reason="one bias value for each partition and bank of tails"):
            nc.sync.dma_start(out=bias[:], in_=b.rearrange("(s p) -> p s", p=P))
        gather_plane(2, 0, S)
        gather_plane(3, 0, S)
        for tile in range(S // TILE):
            project_relations(1, tile)

        gather_plane(4, 0, S)
        interleave_xg(0, 0)
        interleave_xg(0, 1)
        gather_plane(5, 0, S)
        quantize_xg(0, 0)
        quantize_xg(0, 1)
        interleave_weight("we00", True)
        load_weight("wp0", wp, 0, 0)
        interleave_xg(0, 2)
        interleave_xg(0, 3)
        gather_plane(6, 0, S)
        quantize_weight("we00")
        quantize_xg(0, 2)
        quantize_xg(0, 3)
        for tile in range(4):
            project_entities(0, tile, 0)
        interleave_weight("we10", True)
        quantize_weight("we10")

        for quarter in range(2):
            gather_plane(7, QUARTER * quarter, QUARTER * (quarter + 1))
            interleave_xg(1, quarter)
        gather_plane(7, HALF, S)
        interleave_weight("we01", True)
        quantize_xg(1, 0)
        load_weight("wp1", wp, 1, 0)
        quantize_xg(1, 1)
        quantize_weight("we01")

        make_h(0, 0)
        make_h(0, 1)
        interleave_weight("we11", True)
        make_h(0, 2)
        make_h(0, 3)
        for tile in range(4):
            project_entities(1, tile, 0)
        for tile in range(4, 8):
            project_entities(0, tile, 0)
        quantize_weight("we11")
        quantize_h(0, 0, 0, HALF)
        interleave_xg(1, 2)
        interleave_xg(1, 3)
        make_h(1, 0)
        quantize_xg(1, 2)
        make_h(1, 1)
        quantize_xg(1, 3)
        interleave_weight("wp0", False)
        make_h(1, 2)
        make_h(1, 3)
        make_h(0, 4)
        quantize_h(1, 0, 0, HALF)
        quantize_weight("wp0")
        interleave_weight("wp1", False)
        make_h(0, 5)
        make_h(0, 6)
        quantize_weight("wp1")
        make_h(0, 7)
        for tile in range(4, 8):
            project_entities(1, tile, 0)
            make_h(1, tile)
            if tile == 4:
                quantize_h(0, 1, 0, HALF)
            if tile >= 6:
                quantize_h(1, 1, QUARTER * (tile - 6), QUARTER * (tile - 5))

        for part in range(2):
            for s in range(N // P):
                score_triple(0, s, part, start=(part == 0))
        result = w_pool.tile([P, N // P, HALF], F32, name="w_f32", align_bytes=DMA_ALIGN)
        for s in range(N // P):
            score_head(0, s, 0)
            score_head(0, s, 1, stop=True)
            sigmoid(result, s, 0, HALF)
            if s % 2 == 1:
                nc.sync.dma_start(out=out_rows[:, s - 1:s + 1, 0:HALF], in_=result[:, s - 1:s + 1, :])

        for s in range(N // P):
            score_head(1, s, 0, start=True)
        result = w_pool.tile([P, N // P, HALF], F32, name="w_f32", align_bytes=DMA_ALIGN)
        for s in range(N // P):
            score_head(1, s, 1)
            score_triple(1, s, 0)
            score_triple(1, s, 1, stop=True)
            if s < N // P - 1:
                sigmoid(result, s, 0, HALF)
                nc.sync.dma_start(out=out_rows[:, s:s + 1, HALF:S], in_=result[:, s:s + 1, :])
            else:
                for j0, queue in ((0, nc.sync), (QUARTER, nc.scalar)):
                    sigmoid(result, s, j0, j0 + QUARTER)
                    queue.dma_start(out=out_rows[:, s, HALF + j0:HALF + j0 + QUARTER], in_=result[:, s, j0:j0 + QUARTER])
